import numpy as np
import ml_dtypes


def mxq(x, axis, fmt="e4m3"):
    dtype, down = {"e4m3": (ml_dtypes.float8_e4m3fn, 7), "e5m2": (ml_dtypes.float8_e5m2, 14)}[fmt]
    v = np.moveaxis(np.asarray(x, np.float32).astype(ml_dtypes.bfloat16).astype(np.float64), axis, -1)
    blocks = v.reshape(v.shape[:-1] + (-1, 32))
    amax = np.abs(blocks).max(-1, keepdims=True)
    byte = np.maximum(np.where(amax > 0, np.frexp(amax)[1] - 1 + 127, 0) - down, 1)
    scale = np.exp2(byte - 127.0)
    codes = (blocks / scale).astype(np.float32).astype(dtype).astype(np.float64)
    return np.moveaxis((codes * scale).reshape(v.shape), -1, axis)


WIDE = False


def mx_kscale(k):
    if not WIDE:
        return np.ones(k)
    levels = np.array([10, -10, 5, -5, 0])
    if k % 512:
        return np.exp2(np.random.permutation(np.resize(levels, k // 32))).repeat(32)
    a = np.empty((k // 512, 16))
    for p in range(k // 512):
        a[p, :8] = np.random.permutation(np.resize(levels, 8))
        for g in range(8):
            far = levels[np.abs(levels - a[p, g]) >= 10]
            a[p, g + 8] = far[np.random.randint(len(far))]
    return np.exp2(a.ravel()).repeat(32)


def f64(x):
    return np.asarray(x).astype(np.float64)


def striped(idx):
    return np.tile(idx.reshape(-1, 16).T, (8, 1)).astype(np.uint16)


def unstriped(offs):
    return offs[:16].T.reshape(-1).astype(np.int64)


def striped8(idx):
    return np.concatenate([x.reshape(-1, 16).T for x in idx]).astype(np.uint16)


def runs(offs, k):
    lists = np.stack([offs[16 * r : 16 * r + 16].T.reshape(-1) for r in range(8)]).astype(np.int64)
    return lists[np.arange(k) % 512 // 64]


def pack_weight(w):
    k, n = w.shape
    w = f64(np.asarray(w, np.float32).astype(ml_dtypes.bfloat16)).reshape(k // 32, 32, n)
    amax = np.abs(w).max(1)
    byte = np.clip(np.where(amax > 0, np.frexp(amax)[1] - 1 + 127 - 7, 1), 1, 254)
    scaled = (w * np.exp2(127.0 - byte)[:, None, :]).reshape(k, n).astype(np.float32)
    words = np.ascontiguousarray(scaled.reshape(k // 512, 128, 4, n).transpose(0, 1, 3, 2)).astype(ml_dtypes.float8_e4m3fn).view(np.uint8)
    return words, np.ascontiguousarray(byte.astype(np.uint8).reshape(k // 512, 16, n))


def unpack_weight(words, scales):
    g, p, n, _ = words.shape
    vals = np.ascontiguousarray(words).view(ml_dtypes.float8_e4m3fn).astype(np.float64) * np.repeat(np.exp2(scales.astype(np.float64) - 127.0), 8, axis=1)[..., None]
    return vals.transpose(0, 1, 3, 2).reshape(g * 512, n)


def sigmoid(v):
    return 1.0 / (1.0 + np.exp(-np.maximum(v, -700.0)))

def planes(y):
    n, m = y.shape
    v = y.astype(np.float32).astype(ml_dtypes.bfloat16).astype(np.float64).reshape(n // 32, 32, m)
    top = np.abs(v).max(1)
    byte = np.clip(np.where(top > 0, np.frexp(top)[1] - 1 + 127 - 7, 1), 1, 254)
    codes = (v * np.exp2(127.0 - byte)[:, None, :]).reshape(n, m).astype(np.float32).astype(ml_dtypes.float8_e4m3fn).view(np.uint8)
    words = codes.reshape(n // 512, 128, 4, m).transpose(0, 1, 3, 2)
    return np.ascontiguousarray(words), np.ascontiguousarray(byte.astype(np.uint8).reshape(n // 512, 16, m))


K, T, S, N, H, W = 512, 2048, 512, 512, 512, 256


def setup_inputs():
    n = np.random.standard_normal
    s = mx_kscale(K)[:, None]
    u = mx_kscale(H)
    packed_xT = pack_weight(n((K, T)) * s)
    packed_w1 = pack_weight(n((K, H)) / np.sqrt(K) / s)
    packed_w2 = pack_weight(n((H, N)) / np.sqrt(2 * H) / u[:, None])
    packed_w3 = pack_weight(n((K, N)) / np.sqrt(2 * K) / s)
    perm = np.stack([np.random.permutation(S) for _ in range(8)])
    return {
        "x_words": packed_xT[0],
        "x_scales": packed_xT[1],
        "w1_words": packed_w1[0],
        "w1_scales": packed_w1[1],
        "gn": (np.random.uniform(0.5, 1.5, (H, 1)) * u[:, None]).astype(np.float32),
        "w2_words": packed_w2[0],
        "w2_scales": packed_w2[1],
        "w3_words": packed_w3[0],
        "w3_scales": packed_w3[1],
        "offs": striped8(np.random.randint(0, T, (8, S))),
        "n1": striped8(perm[:, :W]),
        "n2": striped8(perm[:, W:]),
        "two": striped(np.random.permutation(T)[:S]),
        "n3": striped(np.random.permutation(S)),
    }


def reference(x_words, x_scales, w1_words, w1_scales, gn, w2_words, w2_scales, w3_words, w3_scales, offs, n1, n2, two, n3):
    xq = unpack_weight(x_words, x_scales)[np.arange(K)[:, None], runs(offs, K)]
    y = unpack_weight(w1_words, w1_scales).T @ xq
    pb = y[np.arange(H)[:, None], runs(n2, H)]
    pa = y[np.arange(H)[:, None], runs(n1, H)]
    rb = pb * sigmoid(pb - pa)
    ra = pa * sigmoid(pa - pb)
    ds = np.zeros((H, S))
    ds[np.arange(H)[:, None], runs(n1, H)] = ra
    dt = ds.copy()
    dt[np.arange(H)[:, None], runs(n2, H)] = rb
    z = f64(gn) * dt
    x_two = unpack_weight(x_words, x_scales)[:, unstriped(two)]
    h = unpack_weight(w2_words, w2_scales).T @ mxq(z, 0, "e4m3") + unpack_weight(w3_words, w3_scales).T @ x_two
    st = h - h[:, unstriped(n3)]
    out_0 = st - (0.5 * st[:, unstriped(n3)])
    return (out_0,) + planes(out_0)

@@ -1,0 +1,240 @@
+from contextlib import ExitStack
+
+import concourse.mybir as mybir
+
+K, T, S, N, H, W = 512, 2048, 512, 512, 512, 256
+FLOPS = 3 * 2 * 512 * 512 * 512
+
+F32 = mybir.dt.float32
+BF16 = mybir.dt.bfloat16
+I32 = mybir.dt.int32
+U32 = mybir.dt.uint32
+U16 = mybir.dt.uint16
+U8 = mybir.dt.uint8
+FP8X4 = mybir.dt.float8_e4m3fn_x4
+ALU = mybir.AluOpType
+ACT = mybir.ActivationFunctionType
+
+P = 128
+PACK = 4
+HALF = S // 2
+LANE = 16
+
+
+def tile_picked_hmixdueltwice_none_po_kernel(
+    tc, x_words, x_scales, w1_words, w1_scales, gn, w2_words, w2_scales, w3_words, w3_scales,
+    offs, n1, n2, two, n3, out_0, out_1, out_2,
+):
+    nc = tc.nc
+
+    def words_of(dram):
+        return dram[0].rearrange("p n t -> p (n t)").bitcast(I32)
+
+    def deal(dst, src):
+        nc.vector.tensor_copy(
+            out=dst.rearrange("p (t m) -> p m t", t=PACK),
+            in_=src.rearrange("p (m t) -> p m t", t=PACK),
+        )
+
+    def load_scale_rows(queues, dst, dram, first):
+        for q in range(4):
+            queues[q].dma_start(
+                out=dst[32 * q + first : 32 * q + first + 4, :].bitcast(I32),
+                in_=dram[0, 4 * q : 4 * q + 4, :].bitcast(I32),
+            )
+
+    def place_scale_rows(queue, dst, src):
+        for q in range(4):
+            queue.dma_start(
+                out=dst[32 * q : 32 * q + 4, :].bitcast(I32),
+                in_=src[32 * q : 32 * q + 32 : 8, :].bitcast(I32),
+            )
+
+    with ExitStack() as ctx:
+        lists = ctx.enter_context(tc.tile_pool(name="lists", bufs=1))
+        keep = ctx.enter_context(tc.tile_pool(name="keep", bufs=1))
+        psum = ctx.enter_context(tc.psum_pool(name="psum", bufs=1))
+
+        offs_t = lists.tile([P, S // LANE], U16, name="offs_t")
+        two_t = lists.tile([P, S // LANE], U16, name="two_t")
+        n1_t = lists.tile([P, W // LANE], U16, name="n1_t")
+        n2_t = lists.tile([P, W // LANE], U16, name="n2_t")
+        n3_t = lists.tile([P, S // LANE], U16, name="n3_t")
+        for tile, dram in ((offs_t, offs), (two_t, two), (n1_t, n1), (n2_t, n2), (n3_t, n3)):
+            nc.sync.dma_start(tile[:], dram)
+
+        x_sc = keep.tile([P, T], U8, name="x_sc")
+        nc.vector.memset(x_sc[:, 0 : T // 2].bitcast(I32), 0)
+        nc.gpsimd.memset(x_sc[:, T // 2 : T].bitcast(I32), 0)
+        nc.scalar.dma_start(out=x_sc[0:P:8, :].bitcast(I32), in_=x_scales[0].bitcast(I32))
+
+        w1_raw = keep.tile([P, H], U32, name="w1_raw", tag="w_raw")
+        nc.sync.dma_start(out=w1_raw[:].bitcast(I32), in_=words_of(w1_words))
+        x_w = keep.tile([P, T], U32, name="x_w")
+        nc.sync.dma_start(out=x_w[:].bitcast(I32), in_=words_of(x_words))
+        w1s_raw = keep.tile([P, H], U8, name="w1s_raw", tag="w2_raw", align_bytes=64)
+        nc.gpsimd.memset(w1s_raw[:].bitcast(I32), 0)
+        load_scale_rows((nc.gpsimd, nc.gpsimd, nc.sync, nc.sync), w1s_raw, w1_scales, 0)
+
+        xq_s = keep.tile([P, S], U8, name="xq_s", align_bytes=64)
+        x2_s = keep.tile([P, S], U8, name="x2_s", align_bytes=64)
+        nc.vector.memset(xq_s[:].bitcast(I32), 0)
+        nc.vector.memset(x2_s[:].bitcast(I32), 0)
+
+        xq_b = keep.tile([P, S], U8, name="xq_b", tag="bytes")
+        nc.vector.tensor_copy(xq_b[:], x_sc[:].indirect(offs_t[:]))
+        place_scale_rows(nc.scalar, xq_s, xq_b)
+
+        w1_w = keep.tile([P, H], U32, name="w1_w", align_bytes=64)
+        deal(w1_w[:].bitcast(I32), w1_raw[:].bitcast(I32))
+        xq_w = keep.tile([P, S], U32, name="xq_w", align_bytes=64)
+        nc.vector.tensor_copy(xq_w[:], x_w[:].indirect(offs_t[:]))
+        w1_s = keep.tile([P, H], U8, name="w1_s", align_bytes=64)
+        deal(w1_s[:], w1s_raw[:])
+
+        y_ps = [psum.tile([P, S], F32, name=f"y_ps{t}") for t in range(PACK)]
+        h_ps = [psum.tile([P, S], F32, name=f"h_ps{t}") for t in range(PACK)]
+        for t in range(PACK):
+            cols = slice(P * t, P * (t + 1))
+            nc.tensor.matmul_mx(
+                out=y_ps[t][:], lhsT=w1_w[:, cols].bitcast(FP8X4), lhsT_scale=w1_s[:, cols],
+                rhs=xq_w[:].bitcast(FP8X4), rhs_scale=xq_s[:], start=True, stop=True,
+            )
+
+        y, pa, pb, diff, sa, sb, dt = [], [], [], [], [], [], []
+        for t in range(PACK):
+            y.append(keep.tile([P, S], F32, name=f"y{t}"))
+            pa.append(keep.tile([P, W], F32, name=f"pa{t}"))
+            pb.append(keep.tile([P, W], F32, name=f"pb{t}"))
+            diff.append(keep.tile([P, W], F32, name=f"diff{t}"))
+            sa.append(keep.tile([P, W], F32, name=f"sa{t}"))
+            sb.append(keep.tile([P, W], F32, name=f"sb{t}", align_bytes=64))
+            dt.append(keep.tile([P, S], F32, name=f"dt{t}"))
+        z_pairs = [keep.tile([P, 2, HALF, 2], BF16, name=f"z_pairs{c}") for c in range(2)]
+        x2_b = keep.tile([P, S], U8, name="x2_b", tag="x2_b")
+        nc.vector.tensor_copy(x2_b[:], x_sc[:].indirect(two_t[:]))
+        place_scale_rows(nc.sync, x2_s, x2_b)
+        gain = keep.tile([P, PACK], F32, name="gain", tag="x2_b")
+        nc.sync.dma_start(out=gain[:], in_=gn.rearrange("(p t) o -> p (t o)", t=PACK))
+
+        def fetch_pairs(t):
+            nc.scalar.activation(y[t][:], y_ps[t][:], ACT.Copy)
+            nc.scalar.activation(pa[t][:], y[t][:].indirect(n1_t[:]), ACT.Copy)
+            nc.scalar.activation(pb[t][:], y[t][:].indirect(n2_t[:]), ACT.Copy)
+            nc.vector.tensor_tensor(diff[t][:], pa[t][:], pb[t][:], ALU.subtract)
+
+        def put_a(t):
+            nc.scalar.activation(sa[t][:], diff[t][:], ACT.Sigmoid)
+            nc.vector.tensor_tensor(dt[t][:].indirect(n1_t[:]), pa[t][:], sa[t][:], ALU.mult)
+
+        def put_b(t):
+            nc.scalar.activation(sb[t][:], diff[t][:], ACT.Sigmoid, scale=-1.0)
+            nc.vector.tensor_tensor(dt[t][:].indirect(n2_t[:]), pb[t][:], sb[t][:], ALU.mult)
+
+        def round_z(t):
+            for c in range(2):
+                nc.scalar.activation(
+                    z_pairs[c][:, t // 2, :, t % 2], dt[t][:, HALF * c : HALF * (c + 1)],
+                    ACT.Copy, scale=gain[:, t : t + 1],
+                )
+
+        fetch_pairs(0)
+        for t in range(PACK):
+            put_a(t)
+            if t + 1 < PACK:
+                fetch_pairs(t + 1)
+            put_b(t)
+        for t in range(PACK):
+            round_z(t)
+
+        x2_w = keep.tile([P, S], U32, name="x2_w", tag="w2_raw", align_bytes=64)
+        nc.vector.tensor_copy(x2_w[:], x_w[:].indirect(two_t[:]))
+        w3_raw = keep.tile([P, N], U32, name="w3_raw", tag="w_raw")
+        nc.sync.dma_start(out=w3_raw[:].bitcast(I32), in_=words_of(w3_words))
+        w3_w = keep.tile([P, N], U32, name="w3_w", align_bytes=64)
+        deal(w3_w[:].bitcast(I32), w3_raw[:].bitcast(I32))
+        w23s_raw = keep.tile([P, N], U8, name="w23s_raw", tag="bytes")
+        nc.gpsimd.memset(w23s_raw[:].bitcast(I32), 0)
+        load_scale_rows((nc.sync,) * 4, w23s_raw, w2_scales, 0)
+        load_scale_rows((nc.sync,) * 4, w23s_raw, w3_scales, 4)
+        w23_s = keep.tile([P, N], U8, name="w23_s", align_bytes=64)
+        deal(w23_s[:], w23s_raw[:])
+        for t in range(PACK):
+            cols = slice(P * t, P * (t + 1))
+            nc.tensor.matmul_mx(
+                out=h_ps[t][:], lhsT=w3_w[:, cols].bitcast(FP8X4), lhsT_scale=w23_s[4:P, cols],
+                rhs=x2_w[:].bitcast(FP8X4), rhs_scale=x2_s[:], start=True, stop=False,
+            )
+        w2_raw = keep.tile([P, N], U32, name="w2_raw", tag="w2_raw", align_bytes=64)
+        nc.sync.dma_start(out=w2_raw[:].bitcast(I32), in_=words_of(w2_words))
+        w2_w = keep.tile([P, N], U32, name="w2_w", tag=f"sb{PACK - 1}", align_bytes=64)
+        deal(w2_w[:].bitcast(I32), w2_raw[:].bitcast(I32))
+
+        z_w, z_s = [], []
+        for c in range(2):
+            z_in = keep.tile([P, HALF * PACK], BF16, name=f"z_in{c}", align_bytes=64)
+            nc.vector.tensor_copy(
+                out=z_in[:].bitcast(I32).rearrange("p (j u) -> p j u", u=2),
+                in_=z_pairs[c][:].rearrange("p u j e -> p (u j e)").bitcast(I32).rearrange("p (u j) -> p j u", u=2),
+            )
+            z_w.append(keep.tile([P, HALF], U32, name=f"z_w{c}", align_bytes=64))
+            z_s.append(keep.tile([P, HALF], U8, name=f"z_s{c}", align_bytes=64))
+            nc.vector.quantize_mx(out=z_w[c][:].bitcast(FP8X4), scales=z_s[c][:], in_=z_in[:])
+        order = (0, 1, 3, 2)
+        for t in order:
+            cols = slice(P * t, P * (t + 1))
+            for c in range(2):
+                nc.tensor.matmul_mx(
+                    out=h_ps[t][:, HALF * c : HALF * (c + 1)], lhsT=w2_w[:, cols].bitcast(FP8X4),
+                    lhsT_scale=w23_s[:, cols], rhs=z_w[c][:].bitcast(FP8X4), rhs_scale=z_s[c][:],
+                    start=False, stop=(c == 1),
+                )
+
+        n3_half = [n3_t[:, (HALF // LANE) * c : (HALF // LANE) * (c + 1)] for c in range(2)]
+        halves = [slice(HALF * c, HALF * (c + 1)) for c in range(2)]
+        res = [keep.tile([P, PACK, HALF], F32, name=f"res{c}") for c in range(2)]
+        st = [keep.tile([P, S], F32, name=f"st{t}") for t in range(PACK)]
+        h = [keep.tile([P, S], F32, name=f"h{t}") for t in range(PACK)]
+        other = [keep.tile([P, S], F32, name=f"other{t}") for t in range(PACK)]
+
+        def st_fused(t):
+            nc.vector.tensor_scalar(h[t][:], other[t][:], -1.0, None, ALU.mult)
+            for c in range(2):
+                nc.vector.tensor_tensor(st[t][:, halves[c]], other[t][:].indirect(n3_half[c]), h[t][:, halves[c]], ALU.add)
+
+        def st_plain(t):
+            nc.scalar.activation(h[t][:], h_ps[t][:], ACT.Copy)
+            for c in range(2):
+                nc.scalar.activation(other[t][:, halves[c]], h[t][:].indirect(n3_half[c]), ACT.Copy)
+            nc.vector.tensor_tensor(st[t][:], h[t][:], other[t][:], ALU.subtract)
+
+        nc.vector.tensor_scalar(other[1][:], h_ps[1][:], -1.0, None, ALU.mult)
+        st_fused(1)
+        st_plain(0)
+        nc.scalar.activation(other[3][:], h_ps[3][:], ACT.Copy, scale=-1.0)
+        st_fused(3)
+        st_plain(2)
+        out_rows = out_0.rearrange("(p t) n -> p t n", t=PACK)
+        out_words = out_1[0].rearrange("p n t -> p (n t)").bitcast(I32)
+        for c in range(2):
+            cols = halves[c]
+            for t in (1, 0, 3, 2):
+                far = keep.tile([P, HALF], F32, name=f"far{c}{t}")
+                nc.scalar.activation(far[:], st[t][:].indirect(n3_half[c]), ACT.Copy)
+                nc.vector.scalar_tensor_tensor(res[c][:, t, :], far[:], -0.5, st[t][:, cols], ALU.mult, ALU.add)
+            nc.sync.dma_start(out=out_rows[:, :, cols], in_=res[c][:])
+            o_in = keep.tile([P, HALF * PACK], BF16, name=f"o_in{c}", align_bytes=64)
+            nc.vector.tensor_copy(
+                out=o_in[:].rearrange("p (j i t) -> p j t i", i=4, t=PACK),
+                in_=res[c][:].rearrange("p t (j i) -> p j t i", i=4),
+            )
+            o_w = keep.tile([P, HALF], U32, name=f"o_w{c}", align_bytes=64)
+            o_s = keep.tile([P, HALF], U8, name=f"o_s{c}", align_bytes=64)
+            nc.vector.quantize_mx(out=o_w[:].bitcast(FP8X4), scales=o_s[:], in_=o_in[:])
+            nc.sync.dma_start(out=out_words[:, cols], in_=o_w[:].bitcast(I32))
+            for q in range(4):
+                queue = nc.sync if q % 2 == 0 else nc.scalar
+                queue.dma_start(
+                    out=out_2[0, 4 * q : 4 * q + 4, cols].bitcast(I32),
+                    in_=o_s[32 * q : 32 * q + 4, :].bitcast(I32),
+                )

@@ -68,6 +68,10 @@ def tile_picked_hmixdueltwice_none_po_kernel(
         nc.gpsimd.memset(x_sc[:, T // 2 : T].bitcast(I32), 0)
         nc.scalar.dma_start(out=x_sc[0:P:8, :].bitcast(I32), in_=x_scales[0].bitcast(I32))
 
+        warm_in = keep.tile([P, 1], F32, name="warm_in")
+        warm_out = keep.tile([P, 1], F32, name="warm_out")
+        nc.vector.memset(warm_in[:], 0.0)
+        nc.scalar.activation(warm_out[:], warm_in[:], ACT.Sigmoid)
         w1_raw = keep.tile([P, H], U32, name="w1_raw", tag="w_raw")
         nc.sync.dma_start(out=w1_raw[:].bitcast(I32), in_=words_of(w1_words))
         x_w = keep.tile([P, T], U32, name="x_w")
@@ -101,9 +105,8 @@ def tile_picked_hmixdueltwice_none_po_kernel(
                 rhs=xq_w[:].bitcast(FP8X4), rhs_scale=xq_s[:], start=True, stop=True,
             )
 
-        y, pa, pb, diff, sa, sb, dt = [], [], [], [], [], [], []
+        pa, pb, diff, sa, sb, dt = [], [], [], [], [], []
         for t in range(PACK):
-            y.append(keep.tile([P, S], F32, name=f"y{t}"))
             pa.append(keep.tile([P, W], F32, name=f"pa{t}"))
             pb.append(keep.tile([P, W], F32, name=f"pb{t}"))
             diff.append(keep.tile([P, W], F32, name=f"diff{t}"))
@@ -117,10 +120,30 @@ def tile_picked_hmixdueltwice_none_po_kernel(
         gain = keep.tile([P, PACK], F32, name="gain", tag="x2_b")
         nc.sync.dma_start(out=gain[:], in_=gn.rearrange("(p t) o -> p (t o)", t=PACK))
 
+        x2_w = keep.tile([P, S], U32, name="x2_w", tag="w2_raw", align_bytes=64)
+        nc.vector.tensor_copy(x2_w[:], x_w[:].indirect(two_t[:]))
+        w3_raw = keep.tile([P, N], U32, name="w3_raw")
+        nc.sync.dma_start(out=w3_raw[:].bitcast(I32), in_=words_of(w3_words))
+        w3_w = keep.tile([P, N], U32, name="w3_w", align_bytes=64)
+        deal(w3_w[:].bitcast(I32), w3_raw[:].bitcast(I32))
+        w23s_raw = keep.tile([P, N], U8, name="w23s_raw", tag="w_raw")
+        nc.gpsimd.memset(w23s_raw[:].bitcast(I32), 0)
+        load_scale_rows((nc.sync,) * 4, w23s_raw, w2_scales, 0)
+        load_scale_rows((nc.sync,) * 4, w23s_raw, w3_scales, 4)
+        w23_s = keep.tile([P, N], U8, name="w23_s", align_bytes=64)
+        deal(w23_s[:], w23s_raw[:])
+        for t in range(PACK):
+            cols = slice(P * t, P * (t + 1))
+            nc.tensor.matmul_mx(
+                out=h_ps[t][:], lhsT=w3_w[:, cols].bitcast(FP8X4), lhsT_scale=w23_s[4:P, cols],
+                rhs=x2_w[:].bitcast(FP8X4), rhs_scale=x2_s[:], start=True, stop=False,
+            )
+
         def fetch_pairs(t):
-            nc.scalar.activation(y[t][:], y_ps[t][:], ACT.Copy)
-            nc.scalar.activation(pa[t][:], y[t][:].indirect(n1_t[:]), ACT.Copy)
-            nc.scalar.activation(pb[t][:], y[t][:].indirect(n2_t[:]), ACT.Copy)
+            y = keep.tile([P, S], F32, name="y")
+            nc.scalar.activation(y[:], y_ps[t][:], ACT.Copy)
+            nc.scalar.activation(pa[t][:], y[:].indirect(n1_t[:]), ACT.Copy)
+            nc.scalar.activation(pb[t][:], y[:].indirect(n2_t[:]), ACT.Copy)
             nc.vector.tensor_tensor(diff[t][:], pa[t][:], pb[t][:], ALU.subtract)
 
         def put_a(t):
@@ -147,25 +170,7 @@ def tile_picked_hmixdueltwice_none_po_kernel(
         for t in range(PACK):
             round_z(t)
 
-        x2_w = keep.tile([P, S], U32, name="x2_w", tag="w2_raw", align_bytes=64)
-        nc.vector.tensor_copy(x2_w[:], x_w[:].indirect(two_t[:]))
-        w3_raw = keep.tile([P, N], U32, name="w3_raw", tag="w_raw")
-        nc.sync.dma_start(out=w3_raw[:].bitcast(I32), in_=words_of(w3_words))
-        w3_w = keep.tile([P, N], U32, name="w3_w", align_bytes=64)
-        deal(w3_w[:].bitcast(I32), w3_raw[:].bitcast(I32))
-        w23s_raw = keep.tile([P, N], U8, name="w23s_raw", tag="bytes")
-        nc.gpsimd.memset(w23s_raw[:].bitcast(I32), 0)
-        load_scale_rows((nc.sync,) * 4, w23s_raw, w2_scales, 0)
-        load_scale_rows((nc.sync,) * 4, w23s_raw, w3_scales, 4)
-        w23_s = keep.tile([P, N], U8, name="w23_s", align_bytes=64)
-        deal(w23_s[:], w23s_raw[:])
-        for t in range(PACK):
-            cols = slice(P * t, P * (t + 1))
-            nc.tensor.matmul_mx(
-                out=h_ps[t][:], lhsT=w3_w[:, cols].bitcast(FP8X4), lhsT_scale=w23_s[4:P, cols],
-                rhs=x2_w[:].bitcast(FP8X4), rhs_scale=x2_s[:], start=True, stop=False,
-            )
-        w2_raw = keep.tile([P, N], U32, name="w2_raw", tag="w2_raw", align_bytes=64)
+        w2_raw = keep.tile([P, N], U32, name="w2_raw", tag="bytes")
         nc.sync.dma_start(out=w2_raw[:].bitcast(I32), in_=words_of(w2_words))
         w2_w = keep.tile([P, N], U32, name="w2_w", tag=f"sb{PACK - 1}", align_bytes=64)
         deal(w2_w[:].bitcast(I32), w2_raw[:].bitcast(I32))
@@ -192,7 +197,6 @@ def tile_picked_hmixdueltwice_none_po_kernel(
 
         n3_half = [n3_t[:, (HALF // LANE) * c : (HALF // LANE) * (c + 1)] for c in range(2)]
         halves = [slice(HALF * c, HALF * (c + 1)) for c in range(2)]
-        res = [keep.tile([P, PACK, HALF], F32, name=f"res{c}") for c in range(2)]
         st = [keep.tile([P, S], F32, name=f"st{t}") for t in range(PACK)]
         h = [keep.tile([P, S], F32, name=f"h{t}") for t in range(PACK)]
         other = [keep.tile([P, S], F32, name=f"other{t}") for t in range(PACK)]
@@ -216,25 +220,27 @@ def tile_picked_hmixdueltwice_none_po_kernel(
         st_plain(2)
         out_rows = out_0.rearrange("(p t) n -> p t n", t=PACK)
         out_words = out_1[0].rearrange("p n t -> p (n t)").bitcast(I32)
-        for c in range(2):
-            cols = halves[c]
+        o_s = keep.tile([P, S], U8, name="o_s", align_bytes=64)
+        for first, width in ((0, 256), (256, 128), (384, 128)):
+            cols = slice(first, first + width)
+            n3_piece = n3_t[:, first // LANE : (first + width) // LANE]
+            res = keep.tile([P, PACK, width], F32, name=f"res{first}")
             for t in (1, 0, 3, 2):
-                far = keep.tile([P, HALF], F32, name=f"far{c}{t}")
-                nc.scalar.activation(far[:], st[t][:].indirect(n3_half[c]), ACT.Copy)
-                nc.vector.scalar_tensor_tensor(res[c][:, t, :], far[:], -0.5, st[t][:, cols], ALU.mult, ALU.add)
-            nc.sync.dma_start(out=out_rows[:, :, cols], in_=res[c][:])
-            o_in = keep.tile([P, HALF * PACK], BF16, name=f"o_in{c}", align_bytes=64)
+                far = keep.tile([P, width], F32, name=f"far{first}_{t}")
+                nc.scalar.activation(far[:], st[t][:].indirect(n3_piece), ACT.Copy)
+                nc.vector.scalar_tensor_tensor(res[:, t, :], far[:], -0.5, st[t][:, cols], ALU.mult, ALU.add)
+            nc.sync.dma_start(out=out_rows[:, :, cols], in_=res[:])
+            o_in = keep.tile([P, width * PACK], BF16, name=f"o_in{first}", align_bytes=64)
             nc.vector.tensor_copy(
                 out=o_in[:].rearrange("p (j i t) -> p j t i", i=4, t=PACK),
-                in_=res[c][:].rearrange("p t (j i) -> p j t i", i=4),
+                in_=res[:].rearrange("p t (j i) -> p j t i", i=4),
             )
-            o_w = keep.tile([P, HALF], U32, name=f"o_w{c}", align_bytes=64)
-            o_s = keep.tile([P, HALF], U8, name=f"o_s{c}", align_bytes=64)
-            nc.vector.quantize_mx(out=o_w[:].bitcast(FP8X4), scales=o_s[:], in_=o_in[:])
+            o_w = keep.tile([P, width], U32, name=f"o_w{first}", align_bytes=64)
+            nc.vector.quantize_mx(out=o_w[:].bitcast(FP8X4), scales=o_s[:, cols], in_=o_in[:])
             nc.sync.dma_start(out=out_words[:, cols], in_=o_w[:].bitcast(I32))
-            for q in range(4):
-                queue = nc.sync if q % 2 == 0 else nc.scalar
-                queue.dma_start(
-                    out=out_2[0, 4 * q : 4 * q + 4, cols].bitcast(I32),
-                    in_=o_s[32 * q : 32 * q + 4, :].bitcast(I32),
-                )
+        for q in range(4):
+            queue = nc.sync if q % 2 == 0 else nc.scalar
+            queue.dma_start(
+                out=out_2[0, 4 * q : 4 * q + 4, :].bitcast(I32),
+                in_=o_s[32 * q : 32 * q + 4, :].bitcast(I32),
+            )

from contextlib import ExitStack

import concourse.mybir as mybir

K, T, S, N, H, W = 512, 2048, 512, 512, 512, 256
FLOPS = 3 * 2 * 512 * 512 * 512

F32 = mybir.dt.float32
BF16 = mybir.dt.bfloat16
I32 = mybir.dt.int32
U32 = mybir.dt.uint32
U16 = mybir.dt.uint16
U8 = mybir.dt.uint8
FP8X4 = mybir.dt.float8_e4m3fn_x4
ALU = mybir.AluOpType
ACT = mybir.ActivationFunctionType

P = 128
PACK = 4
HALF = S // 2
LANE = 16


def tile_picked_hmixdueltwice_none_po_kernel(
    tc, x_words, x_scales, w1_words, w1_scales, gn, w2_words, w2_scales, w3_words, w3_scales,
    offs, n1, n2, two, n3, out_0, out_1, out_2,
):
    nc = tc.nc

    def words_of(dram):
        return dram[0].rearrange("p n t -> p (n t)").bitcast(I32)

    def deal(dst, src):
        nc.vector.tensor_copy(
            out=dst.rearrange("p (t m) -> p m t", t=PACK),
            in_=src.rearrange("p (m t) -> p m t", t=PACK),
        )

    def load_scale_rows(queues, dst, dram, first):
        for q in range(4):
            queues[q].dma_start(
                out=dst[32 * q + first : 32 * q + first + 4, :].bitcast(I32),
                in_=dram[0, 4 * q : 4 * q + 4, :].bitcast(I32),
            )

    def place_scale_rows(queue, dst, src):
        for q in range(4):
            queue.dma_start(
                out=dst[32 * q : 32 * q + 4, :].bitcast(I32),
                in_=src[32 * q : 32 * q + 32 : 8, :].bitcast(I32),
            )

    with ExitStack() as ctx:
        lists = ctx.enter_context(tc.tile_pool(name="lists", bufs=1))
        keep = ctx.enter_context(tc.tile_pool(name="keep", bufs=1))
        psum = ctx.enter_context(tc.psum_pool(name="psum", bufs=1))

        offs_t = lists.tile([P, S // LANE], U16, name="offs_t")
        two_t = lists.tile([P, S // LANE], U16, name="two_t")
        n1_t = lists.tile([P, W // LANE], U16, name="n1_t")
        n2_t = lists.tile([P, W // LANE], U16, name="n2_t")
        n3_t = lists.tile([P, S // LANE], U16, name="n3_t")
        for tile, dram in ((offs_t, offs), (two_t, two), (n1_t, n1), (n2_t, n2), (n3_t, n3)):
            nc.sync.dma_start(tile[:], dram)

        x_sc = keep.tile([P, T], U8, name="x_sc")
        nc.vector.memset(x_sc[:, 0 : T // 2].bitcast(I32), 0)
        nc.gpsimd.memset(x_sc[:, T // 2 : T].bitcast(I32), 0)
        nc.scalar.dma_start(out=x_sc[0:P:8, :].bitcast(I32), in_=x_scales[0].bitcast(I32))

        warm_in = keep.tile([P, 1], F32, name="warm_in")
        warm_out = keep.tile([P, 1], F32, name="warm_out")
        nc.vector.memset(warm_in[:], 0.0)
        nc.scalar.activation(warm_out[:], warm_in[:], ACT.Sigmoid)
        w1_raw = keep.tile([P, H], U32, name="w1_raw", tag="w_raw")
        nc.sync.dma_start(out=w1_raw[:].bitcast(I32), in_=words_of(w1_words))
        x_w = keep.tile([P, T], U32, name="x_w")
        nc.sync.dma_start(out=x_w[:].bitcast(I32), in_=words_of(x_words))
        w1s_raw = keep.tile([P, H], U8, name="w1s_raw", tag="w2_raw", align_bytes=64)
        nc.gpsimd.memset(w1s_raw[:].bitcast(I32), 0)
        load_scale_rows((nc.gpsimd, nc.gpsimd, nc.sync, nc.sync), w1s_raw, w1_scales, 0)

        xq_s = keep.tile([P, S], U8, name="xq_s", align_bytes=64)
        x2_s = keep.tile([P, S], U8, name="x2_s", align_bytes=64)
        nc.vector.memset(xq_s[:].bitcast(I32), 0)
        nc.vector.memset(x2_s[:].bitcast(I32), 0)

        xq_b = keep.tile([P, S], U8, name="xq_b", tag="bytes")
        nc.vector.tensor_copy(xq_b[:], x_sc[:].indirect(offs_t[:]))
        place_scale_rows(nc.scalar, xq_s, xq_b)

        w1_w = keep.tile([P, H], U32, name="w1_w", align_bytes=64)
        deal(w1_w[:].bitcast(I32), w1_raw[:].bitcast(I32))
        xq_w = keep.tile([P, S], U32, name="xq_w", align_bytes=64)
        nc.vector.tensor_copy(xq_w[:], x_w[:].indirect(offs_t[:]))
        w1_s = keep.tile([P, H], U8, name="w1_s", align_bytes=64)
        deal(w1_s[:], w1s_raw[:])

        y_ps = [psum.tile([P, S], F32, name=f"y_ps{t}") for t in range(PACK)]
        h_ps = [psum.tile([P, S], F32, name=f"h_ps{t}") for t in range(PACK)]
        for t in range(PACK):
            cols = slice(P * t, P * (t + 1))
            nc.tensor.matmul_mx(
                out=y_ps[t][:], lhsT=w1_w[:, cols].bitcast(FP8X4), lhsT_scale=w1_s[:, cols],
                rhs=xq_w[:].bitcast(FP8X4), rhs_scale=xq_s[:], start=True, stop=True,
            )

        pa, pb, diff, sa, sb, dt = [], [], [], [], [], []
        for t in range(PACK):
            pa.append(keep.tile([P, W], F32, name=f"pa{t}"))
            pb.append(keep.tile([P, W], F32, name=f"pb{t}"))
            diff.append(keep.tile([P, W], F32, name=f"diff{t}"))
            sa.append(keep.tile([P, W], F32, name=f"sa{t}"))
            sb.append(keep.tile([P, W], F32, name=f"sb{t}", align_bytes=64))
            dt.append(keep.tile([P, S], F32, name=f"dt{t}"))
        z_pairs = [keep.tile([P, 2, HALF, 2], BF16, name=f"z_pairs{c}") for c in range(2)]
        x2_b = keep.tile([P, S], U8, name="x2_b", tag="x2_b")
        nc.vector.tensor_copy(x2_b[:], x_sc[:].indirect(two_t[:]))
        place_scale_rows(nc.sync, x2_s, x2_b)
        gain = keep.tile([P, PACK], F32, name="gain", tag="x2_b")
        nc.sync.dma_start(out=gain[:], in_=gn.rearrange("(p t) o -> p (t o)", t=PACK))

        x2_w = keep.tile([P, S], U32, name="x2_w", tag="w2_raw", align_bytes=64)
        nc.vector.tensor_copy(x2_w[:], x_w[:].indirect(two_t[:]))
        w3_raw = keep.tile([P, N], U32, name="w3_raw")
        nc.sync.dma_start(out=w3_raw[:].bitcast(I32), in_=words_of(w3_words))
        w3_w = keep.tile([P, N], U32, name="w3_w", align_bytes=64)
        deal(w3_w[:].bitcast(I32), w3_raw[:].bitcast(I32))
        w23s_raw = keep.tile([P, N], U8, name="w23s_raw", tag="w_raw")
        nc.gpsimd.memset(w23s_raw[:].bitcast(I32), 0)
        load_scale_rows((nc.sync,) * 4, w23s_raw, w2_scales, 0)
        load_scale_rows((nc.sync,) * 4, w23s_raw, w3_scales, 4)
        w23_s = keep.tile([P, N], U8, name="w23_s", align_bytes=64)
        deal(w23_s[:], w23s_raw[:])
        for t in range(PACK):
            cols = slice(P * t, P * (t + 1))
            nc.tensor.matmul_mx(
                out=h_ps[t][:], lhsT=w3_w[:, cols].bitcast(FP8X4), lhsT_scale=w23_s[4:P, cols],
                rhs=x2_w[:].bitcast(FP8X4), rhs_scale=x2_s[:], start=True, stop=False,
            )

        def fetch_pairs(t):
            y = keep.tile([P, S], F32, name="y")
            nc.scalar.activation(y[:], y_ps[t][:], ACT.Copy)
            nc.scalar.activation(pa[t][:], y[:].indirect(n1_t[:]), ACT.Copy)
            nc.scalar.activation(pb[t][:], y[:].indirect(n2_t[:]), ACT.Copy)
            nc.vector.tensor_tensor(diff[t][:], pa[t][:], pb[t][:], ALU.subtract)

        def put_a(t):
            nc.scalar.activation(sa[t][:], diff[t][:], ACT.Sigmoid)
            nc.vector.tensor_tensor(dt[t][:].indirect(n1_t[:]), pa[t][:], sa[t][:], ALU.mult)

        def put_b(t):
            nc.scalar.activation(sb[t][:], diff[t][:], ACT.Sigmoid, scale=-1.0)
            nc.vector.tensor_tensor(dt[t][:].indirect(n2_t[:]), pb[t][:], sb[t][:], ALU.mult)

        def round_z(t):
            for c in range(2):
                nc.scalar.activation(
                    z_pairs[c][:, t // 2, :, t % 2], dt[t][:, HALF * c : HALF * (c + 1)],
                    ACT.Copy, scale=gain[:, t : t + 1],
                )

        fetch_pairs(0)
        for t in range(PACK):
            put_a(t)
            if t + 1 < PACK:
                fetch_pairs(t + 1)
            put_b(t)
        for t in range(PACK):
            round_z(t)

        w2_raw = keep.tile([P, N], U32, name="w2_raw", tag="bytes")
        nc.sync.dma_start(out=w2_raw[:].bitcast(I32), in_=words_of(w2_words))
        w2_w = keep.tile([P, N], U32, name="w2_w", tag=f"sb{PACK - 1}", align_bytes=64)
        deal(w2_w[:].bitcast(I32), w2_raw[:].bitcast(I32))

        z_w, z_s = [], []
        for c in range(2):
            z_in = keep.tile([P, HALF * PACK], BF16, name=f"z_in{c}", align_bytes=64)
            nc.vector.tensor_copy(
                out=z_in[:].bitcast(I32).rearrange("p (j u) -> p j u", u=2),
                in_=z_pairs[c][:].rearrange("p u j e -> p (u j e)").bitcast(I32).rearrange("p (u j) -> p j u", u=2),
            )
            z_w.append(keep.tile([P, HALF], U32, name=f"z_w{c}", align_bytes=64))
            z_s.append(keep.tile([P, HALF], U8, name=f"z_s{c}", align_bytes=64))
            nc.vector.quantize_mx(out=z_w[c][:].bitcast(FP8X4), scales=z_s[c][:], in_=z_in[:])
        order = (0, 1, 3, 2)
        for t in order:
            cols = slice(P * t, P * (t + 1))
            for c in range(2):
                nc.tensor.matmul_mx(
                    out=h_ps[t][:, HALF * c : HALF * (c + 1)], lhsT=w2_w[:, cols].bitcast(FP8X4),
                    lhsT_scale=w23_s[:, cols], rhs=z_w[c][:].bitcast(FP8X4), rhs_scale=z_s[c][:],
                    start=False, stop=(c == 1),
                )

        n3_half = [n3_t[:, (HALF // LANE) * c : (HALF // LANE) * (c + 1)] for c in range(2)]
        halves = [slice(HALF * c, HALF * (c + 1)) for c in range(2)]
        st = [keep.tile([P, S], F32, name=f"st{t}") for t in range(PACK)]
        h = [keep.tile([P, S], F32, name=f"h{t}") for t in range(PACK)]
        other = [keep.tile([P, S], F32, name=f"other{t}") for t in range(PACK)]

        def st_fused(t):
            nc.vector.tensor_scalar(h[t][:], other[t][:], -1.0, None, ALU.mult)
            for c in range(2):
                nc.vector.tensor_tensor(st[t][:, halves[c]], other[t][:].indirect(n3_half[c]), h[t][:, halves[c]], ALU.add)

        def st_plain(t):
            nc.scalar.activation(h[t][:], h_ps[t][:], ACT.Copy)
            for c in range(2):
                nc.scalar.activation(other[t][:, halves[c]], h[t][:].indirect(n3_half[c]), ACT.Copy)
            nc.vector.tensor_tensor(st[t][:], h[t][:], other[t][:], ALU.subtract)

        nc.vector.tensor_scalar(other[1][:], h_ps[1][:], -1.0, None, ALU.mult)
        st_fused(1)
        st_plain(0)
        nc.scalar.activation(other[3][:], h_ps[3][:], ACT.Copy, scale=-1.0)
        st_fused(3)
        st_plain(2)
        out_rows = out_0.rearrange("(p t) n -> p t n", t=PACK)
        out_words = out_1[0].rearrange("p n t -> p (n t)").bitcast(I32)
        o_s = keep.tile([P, S], U8, name="o_s", align_bytes=64)
        for first, width in ((0, 256), (256, 128), (384, 128)):
            cols = slice(first, first + width)
            n3_piece = n3_t[:, first // LANE : (first + width) // LANE]
            res = keep.tile([P, PACK, width], F32, name=f"res{first}")
            for t in (1, 0, 3, 2):
                far = keep.tile([P, width], F32, name=f"far{first}_{t}")
                nc.scalar.activation(far[:], st[t][:].indirect(n3_piece), ACT.Copy)
                nc.vector.scalar_tensor_tensor(res[:, t, :], far[:], -0.5, st[t][:, cols], ALU.mult, ALU.add)
            nc.sync.dma_start(out=out_rows[:, :, cols], in_=res[:])
            o_in = keep.tile([P, width * PACK], BF16, name=f"o_in{first}", align_bytes=64)
            nc.vector.tensor_copy(
                out=o_in[:].rearrange("p (j i t) -> p j t i", i=4, t=PACK),
                in_=res[:].rearrange("p t (j i) -> p j t i", i=4),
            )
            o_w = keep.tile([P, width], U32, name=f"o_w{first}", align_bytes=64)
            nc.vector.quantize_mx(out=o_w[:].bitcast(FP8X4), scales=o_s[:, cols], in_=o_in[:])
            nc.sync.dma_start(out=out_words[:, cols], in_=o_w[:].bitcast(I32))
        for q in range(4):
            queue = nc.sync if q % 2 == 0 else nc.scalar
            queue.dma_start(
                out=out_2[0, 4 * q : 4 * q + 4, :].bitcast(I32),
                in_=o_s[32 * q : 32 * q + 4, :].bitcast(I32),
            )
